import numpy as np
import ml_dtypes


def mxq(x, axis, fmt="e4m3"):
    dtype, down = {"e4m3": (ml_dtypes.float8_e4m3fn, 7), "e5m2": (ml_dtypes.float8_e5m2, 14)}[fmt]
    v = np.moveaxis(np.asarray(x, np.float32).astype(ml_dtypes.bfloat16).astype(np.float64), axis, -1)
    blocks = v.reshape(v.shape[:-1] + (-1, 32))
    amax = np.abs(blocks).max(-1, keepdims=True)
    byte = np.maximum(np.where(amax > 0, np.frexp(amax)[1] - 1 + 127, 0) - down, 1)
    scale = np.exp2(byte - 127.0)
    codes = (blocks / scale).astype(np.float32).astype(dtype).astype(np.float64)
    return np.moveaxis((codes * scale).reshape(v.shape), -1, axis)


WIDE = False


def mx_kscale(k):
    if not WIDE:
        return np.ones(k)
    levels = np.array([10, -10, 5, -5, 0])
    if k % 512:
        return np.exp2(np.random.permutation(np.resize(levels, k // 32))).repeat(32)
    a = np.empty((k // 512, 16))
    for p in range(k // 512):
        a[p, :8] = np.random.permutation(np.resize(levels, 8))
        for g in range(8):
            far = levels[np.abs(levels - a[p, g]) >= 10]
            a[p, g + 8] = far[np.random.randint(len(far))]
    return np.exp2(a.ravel()).repeat(32)


def f64(x):
    return np.asarray(x).astype(np.float64)


def striped(idx):
    return np.tile(idx.reshape(-1, 16).T, (8, 1)).astype(np.uint16)


def unstriped(offs):
    return offs[:16].T.reshape(-1).astype(np.int64)


def pack_weight(w):
    k, n = w.shape
    w = f64(np.asarray(w, np.float32).astype(ml_dtypes.bfloat16)).reshape(k // 32, 32, n)
    amax = np.abs(w).max(1)
    byte = np.clip(np.where(amax > 0, np.frexp(amax)[1] - 1 + 127 - 7, 1), 1, 254)
    scaled = (w * np.exp2(127.0 - byte)[:, None, :]).reshape(k, n).astype(np.float32)
    words = np.ascontiguousarray(scaled.reshape(k // 512, 128, 4, n).transpose(0, 1, 3, 2)).astype(ml_dtypes.float8_e4m3fn).view(np.uint8)
    return words, np.ascontiguousarray(byte.astype(np.uint8).reshape(k // 512, 16, n))


def unpack_weight(words, scales):
    g, p, n, _ = words.shape
    vals = np.ascontiguousarray(words).view(ml_dtypes.float8_e4m3fn).astype(np.float64) * np.repeat(np.exp2(scales.astype(np.float64) - 127.0), 8, axis=1)[..., None]
    return vals.transpose(0, 1, 3, 2).reshape(g * 512, n)


K, T, S, H, V, W, G, U = 1024, 2048, 512, 512, 256, 1024, 1024, 512
P = 2 ** 7


def setup_inputs():
    n = np.random.standard_normal
    s = mx_kscale(K)[:, None]
    u = mx_kscale(H)
    packed_xT = pack_weight(n((K, T)) * s)
    packed_eT = pack_weight(n((H, W)) / np.sqrt(H) / u[:, None])
    packed_dT = pack_weight(n((H, G)) / np.sqrt(H) / u[:, None])
    return {
        "x_words": packed_xT[0],
        "x_scales": packed_xT[1],
        "w1": (n((K, H)) / np.sqrt(K) / s * u).astype(np.float32),
        "e_words": packed_eT[0],
        "e_scales": packed_eT[1],
        "d_words": packed_dT[0],
        "d_scales": packed_dT[1],
        "ms": (np.tile(0.3 * n(G), (P, 1))).astype(np.float32),
        "isp": (np.tile(np.random.uniform(0.7, 1.4, G), (P, 1))).astype(np.float32),
        "offs": striped(np.random.permutation(T)[:S]),
        "coh": striped(np.random.permutation(W)[:U]),
        "spk": striped(np.random.permutation(G)[:V]),
    }


def reference(x_words, x_scales, w1, e_words, e_scales, d_words, d_scales, ms, isp, offs, coh, spk):
    xq = unpack_weight(x_words, x_scales)[:, unstriped(offs)]
    h = mxq(f64(w1), 0, "e4m3").T @ xq
    hq = mxq(h, 0, "e4m3")
    d_spk = unpack_weight(d_words, d_scales)[:, unstriped(spk)]
    y = hq.T @ d_spk
    e_coh = unpack_weight(e_words, e_scales)[:, unstriped(coh)]
    z = hq.T @ e_coh
    mean = z.mean(axis=1, keepdims=True)
    dz = z - mean
    d2 = (dz) ** 2
    sd = np.sqrt(d2.mean(axis=1, keepdims=True) + 0.01)
    nz = (y - mean) / sd
    return 0.5 * (nz + (y - (f64(ms)[:1][:, unstriped(spk)])) * (f64(isp)[:1][:, unstriped(spk)]))

@@ -1,0 +1,185 @@
+from contextlib import ExitStack
+
+import concourse.mybir as mybir
+from concourse.masks import make_identity
+
+K, T, S, H, V, W, G, U = 1024, 2048, 512, 512, 256, 1024, 1024, 512
+FLOPS = 2 * K * H * S + 2 * H * S * (V + U)
+
+F32 = mybir.dt.float32
+BF16 = mybir.dt.bfloat16
+I32 = mybir.dt.int32
+U32 = mybir.dt.uint32
+U16 = mybir.dt.uint16
+U8 = mybir.dt.uint8
+FP8X4 = mybir.dt.float8_e4m3fn_x4
+ACT = mybir.ActivationFunctionType
+ALU = mybir.AluOpType
+
+P = 128
+PACK = 4
+PASSES = K // (P * PACK)
+TILES = S // P
+HALF = S // 2
+EPS = 0.01
+
+
+def tile_picked_ysnorm_sym_p_kernel(
+    tc, x_words, x_scales, w1, e_words, e_scales, d_words, d_scales, ms, isp, offs, coh, spk, out
+):
+    nc = tc.nc
+    with ExitStack() as ctx:
+        keep = ctx.enter_context(tc.tile_pool(name="keep", bufs=1))
+        psum = ctx.enter_context(tc.psum_pool(name="psum", bufs=1))
+
+        def sb(shape, dtype, name):
+            return keep.tile(shape, dtype, name=name, align_bytes=64)
+
+        offs_sb = keep.tile([P, S // 16], U16, name="offs_sb")
+        coh_sb = keep.tile([P, U // 16], U16, name="coh_sb")
+        spk_sb = keep.tile([P, V // 16], U16, name="spk_sb")
+        w_raw = [sb([P, PACK, H], F32, f"w_raw{o}") for o in range(PASSES)]
+        x_tab = [sb([P, T], I32, f"x_tab{o}") for o in range(PASSES)]
+        e_tab = sb([P, W], I32, "e_tab")
+        d_tab = sb([P, G], I32, "d_tab")
+        xs_tab = sb([P, T], U8, "xs_tab")
+        es_tab = sb([P, W], U8, "es_tab")
+        ds_tab = sb([P, G], U8, "ds_tab")
+        stat_tab = sb([P, G], F32, "stat_tab")
+        ident = sb([P, P], F32, "ident")
+
+        def words(dram):
+            return dram.rearrange("p n t -> p (n t)").bitcast(I32)
+
+        nc.vector.memset(stat_tab[:], 0.0)
+        nc.vector.memset(ds_tab[:].bitcast(I32), 0)
+        nc.gpsimd.memset(xs_tab[:].bitcast(I32), 0)
+        make_identity(nc, ident[:])
+
+        def load_w(o):
+            nc.sync.dma_start(w_raw[o][:], w1[512 * o : 512 * (o + 1), :].rearrange("(p r) c -> p r c", r=PACK))
+
+        for q in range(4):
+            rows = e_scales[0, 4 * q : 4 * q + 4, :].bitcast(I32)
+            nc.scalar.dma_start(es_tab[32 * q : 32 * q + 32, :].bitcast(I32), rows.unsqueeze(0).broadcast_to([8, 4, W // 4]))
+        for q in range(4):
+            nc.gpsimd.dma_start(xs_tab[32 * q : 32 * q + 8, :].bitcast(I32), x_scales[:, 4 * q : 4 * q + 4, :].bitcast(I32))
+        nc.sync.dma_start(coh_sb[:], coh)
+        load_w(0)
+        nc.sync.dma_start(offs_sb[:], offs)
+        load_w(1)
+        nc.sync.dma_start(spk_sb[:], spk)
+        nc.sync.dma_start(stat_tab[0:1, :], ms[0:1, :])
+        nc.sync.dma_start(stat_tab[1:2, :], isp[0:1, :])
+        nc.sync.dma_start(x_tab[0][:], words(x_words[0]))
+        for q in range(4):
+            nc.sync.dma_start(ds_tab[32 * q : 32 * q + 4, :].bitcast(I32), d_scales[0, 4 * q : 4 * q + 4, :].bitcast(I32))
+        nc.sync.dma_start(x_tab[1][:], words(x_words[1]))
+        nc.sync.dma_start(e_tab[:], words(e_words[0]))
+        nc.sync.dma_start(d_tab[:], words(d_words[0]))
+
+        half = sb([P, 1], F32, "half")
+        nc.scalar.activation(half[:], ident[:, 0:1], ACT.Abs_reciprocal_sqrt, bias=4.0, scale=0.0)
+
+        es_g = sb([P, U], U8, "es_g")
+        ds_g = sb([P, V], U8, "ds_g")
+        xs_g = sb([P, S], U8, "xs_g")
+        stat_g = sb([P, V], F32, "stat_g")
+        nc.vector.tensor_copy(es_g[:], es_tab[:].indirect(coh_sb[:]))
+        nc.vector.tensor_copy(ds_g[:], ds_tab[:].indirect(spk_sb[:]))
+        nc.vector.tensor_copy(xs_g[:], xs_tab[:].indirect(offs_sb[:]))
+        nc.vector.tensor_copy(stat_g[:], stat_tab[:].indirect(spk_sb[:]))
+
+        w_codes = [sb([P, H], U32, f"w_codes{o}") for o in range(PASSES)]
+        w_sc = [sb([P, H], U8, f"w_sc{o}") for o in range(PASSES)]
+        for o in range(PASSES):
+            w_bf = sb([P, PACK * H], BF16, f"w_bf{o}")
+            nc.scalar.copy(
+                w_bf[:].rearrange("p (j m r) -> p m r j", j=PACK, r=PACK),
+                w_raw[o][:].rearrange("p r (m j) -> p m r j", j=PACK),
+            )
+            nc.vector.quantize_mx(out=w_codes[o][:].bitcast(FP8X4), scales=w_sc[o][:], in_=w_bf[:])
+
+        turned = psum.tile([P, PACK, P], F32, name="turned", tag="h", bufs=2)
+        for vh in range(2):
+            nc.tensor.transpose(turned[:, vh, :], stat_g[:, vh * P : (vh + 1) * P], ident[:])
+        cols = sb([P, 4], F32, "cols")
+        nc.scalar.activation(cols[:, 0:2], turned[:, 0:2, 1], ACT.Copy, scale=half[:])
+        for vh in range(2):
+            nc.scalar.activation(cols[:, 2 + vh : 3 + vh], turned[:, vh, 0:1], ACT.Copy, scale=cols[:, vh : vh + 1])
+        spread = psum.tile([P, 2 * V], F32, name="spread")
+        for c in range(4):
+            nc.tensor.transpose(spread[:, c * P : (c + 1) * P], cols[:, c : c + 1].to_broadcast([P, P]), ident[:])
+        gain = sb([P, V], F32, "gain")
+        nc.scalar.copy(gain[:], spread[:, 0:V])
+        shift = spread[:, V : 2 * V]
+
+        x_g = [sb([P, S], U32, f"x_g{o}") for o in range(PASSES)]
+        nc.vector.tensor_copy(x_g[0][:], x_tab[0][:].bitcast(U32).indirect(offs_sb[:]))
+        for hf in range(2):
+            cut = slice(hf * HALF // 16, (hf + 1) * HALF // 16)
+            nc.vector.tensor_copy(x_g[1][:, hf * HALF : (hf + 1) * HALF], x_tab[1][:].bitcast(U32).indirect(offs_sb[:, cut]))
+        e_g = sb([P, U], U32, "e_g")
+        d_g = sb([P, V], U32, "d_g")
+        nc.vector.tensor_copy(e_g[:], e_tab[:].bitcast(U32).indirect(coh_sb[:]))
+        nc.vector.tensor_copy(d_g[:], d_tab[:].bitcast(U32).indirect(spk_sb[:]))
+
+        h_codes, h_sc, zs, ys = {}, {}, {}, {}
+
+        def hidden(t):
+            h_ps = psum.tile([P, PACK, P], F32, name=f"h_ps{t}", tag="h", bufs=2)
+            tok = slice(t * P, (t + 1) * P)
+            for j in range(PACK):
+                ch = slice(j * P, (j + 1) * P)
+                for o in range(PASSES):
+                    nc.tensor.matmul_mx(
+                        out=h_ps[:, j, :],
+                        lhsT=w_codes[o][:, ch].bitcast(FP8X4),
+                        lhsT_scale=w_sc[o][:, ch],
+                        rhs=x_g[o][:, tok].bitcast(FP8X4),
+                        rhs_scale=xs_g[4 * o : P, tok],
+                        start=(o == 0),
+                        stop=(o == PASSES - 1),
+                    )
+            h_bf = sb([P, P * PACK], BF16, f"h_bf{t}")
+            nc.scalar.copy(h_bf[:].rearrange("p (n j) -> p n j", j=PACK), h_ps[:].rearrange("p j n -> p n j"))
+            h_codes[t] = sb([P, P], U32, f"h_codes{t}")
+            h_sc[t] = sb([P, P], U8, f"h_sc{t}")
+            nc.vector.quantize_mx(out=h_codes[t][:].bitcast(FP8X4), scales=h_sc[t][:], in_=h_bf[:])
+
+        def scores(t):
+            zs[t] = psum.tile([P, U], F32, name=f"z_ps{t}", tag="z", bufs=3)
+            ys[t] = psum.tile([P, V], F32, name=f"y_ps{t}", tag="y", bufs=2)
+            for acc, codes, sc in ((zs[t], e_g, es_g), (ys[t], d_g, ds_g)):
+                nc.tensor.matmul_mx(
+                    out=acc[:],
+                    lhsT=h_codes[t][:].bitcast(FP8X4),
+                    lhsT_scale=h_sc[t][:],
+                    rhs=codes[:].bitcast(FP8X4),
+                    rhs_scale=sc[:],
+                    start=True,
+                    stop=True,
+                )
+
+        def finish(t):
+            bn = sb([P, 6], F32, f"bn{t}")
+            mv = sb([P, 2], F32, f"mv{t}")
+            inv = sb([P, 1], F32, f"inv{t}")
+            off = sb([P, 1], F32, f"off{t}")
+            scaled = sb([P, V], F32, f"scaled{t}")
+            res = sb([P, V], F32, f"res{t}")
+            nc.vector.bn_stats(bn[:], zs[t][:])
+            nc.vector.bn_aggr(mv[:], bn[:])
+            nc.scalar.activation(inv[:], mv[:, 1:2], ACT.Abs_reciprocal_sqrt, bias=4.0 * EPS, scale=4.0)
+            nc.scalar.activation(off[:], mv[:, 0:1], ACT.Copy, scale=inv[:])
+            nc.vector.scalar_tensor_tensor(scaled[:], gain[:], inv[:], ys[t][:], ALU.add, ALU.mult)
+            nc.vector.scalar_tensor_tensor(res[:], scaled[:], off[:], shift, ALU.subtract, ALU.subtract)
+            nc.sync.dma_start(out[t * P : (t + 1) * P, :], res[:])
+
+        for step in range(TILES + 2):
+            if step < TILES:
+                hidden(step)
+            if 1 <= step <= TILES:
+                scores(step - 1)
+            if step >= 2:
+                finish(step - 2)

@@ -22,6 +22,7 @@ PASSES = K // (P * PACK)
 TILES = S // P
 HALF = S // 2
 EPS = 0.01
+SCALAR_STATS = (2,)
 
 
 def tile_picked_ysnorm_sym_p_kernel(
@@ -32,54 +33,52 @@ def tile_picked_ysnorm_sym_p_kernel(
         keep = ctx.enter_context(tc.tile_pool(name="keep", bufs=1))
         psum = ctx.enter_context(tc.psum_pool(name="psum", bufs=1))
 
-        def sb(shape, dtype, name):
-            return keep.tile(shape, dtype, name=name, align_bytes=64)
+        def sb(shape, dtype, name, tag=None):
+            return keep.tile(shape, dtype, name=name, tag=tag or name, align_bytes=64)
 
         offs_sb = keep.tile([P, S // 16], U16, name="offs_sb")
         coh_sb = keep.tile([P, U // 16], U16, name="coh_sb")
         spk_sb = keep.tile([P, V // 16], U16, name="spk_sb")
-        w_raw = [sb([P, PACK, H], F32, f"w_raw{o}") for o in range(PASSES)]
-        x_tab = [sb([P, T], I32, f"x_tab{o}") for o in range(PASSES)]
-        e_tab = sb([P, W], I32, "e_tab")
-        d_tab = sb([P, G], I32, "d_tab")
+        w_raw = [sb([P, PACK, H], F32, f"w_raw{o}", tag=f"raw{o}") for o in range(PASSES)]
         xs_tab = sb([P, T], U8, "xs_tab")
-        es_tab = sb([P, W], U8, "es_tab")
-        ds_tab = sb([P, G], U8, "ds_tab")
-        stat_tab = sb([P, G], F32, "stat_tab")
+        es_tab = sb([P, W], U8, "es_tab", tag="es")
+        stat_tab = sb([P, G], F32, "stat_tab", tag="stat")
         ident = sb([P, P], F32, "ident")
+        four = sb([P, 1], F32, "four")
+        ds_tab = sb([P, G], U8, "ds_tab", tag="ds")
 
         def words(dram):
             return dram.rearrange("p n t -> p (n t)").bitcast(I32)
 
-        nc.vector.memset(stat_tab[:], 0.0)
-        nc.vector.memset(ds_tab[:].bitcast(I32), 0)
-        nc.gpsimd.memset(xs_tab[:].bitcast(I32), 0)
-        make_identity(nc, ident[:])
-
         def load_w(o):
             nc.sync.dma_start(w_raw[o][:], w1[512 * o : 512 * (o + 1), :].rearrange("(p r) c -> p r c", r=PACK))
 
-        for q in range(4):
-            rows = e_scales[0, 4 * q : 4 * q + 4, :].bitcast(I32)
-            nc.scalar.dma_start(es_tab[32 * q : 32 * q + 32, :].bitcast(I32), rows.unsqueeze(0).broadcast_to([8, 4, W // 4]))
-        for q in range(4):
-            nc.gpsimd.dma_start(xs_tab[32 * q : 32 * q + 8, :].bitcast(I32), x_scales[:, 4 * q : 4 * q + 4, :].bitcast(I32))
+        def load_scale_rows(tab, scales):
+            for q in range(4):
+                rows = scales[0, 4 * q : 4 * q + 4, :].bitcast(I32)
+                nc.sync.dma_start(tab[32 * q : 32 * q + 32, :].bitcast(I32), rows.unsqueeze(0).broadcast_to([8, 4, W // 4]))
+
+        nc.vector.memset(stat_tab[:], 0.0)
+        nc.vector.memset(xs_tab[:].bitcast(I32), 0)
+        nc.vector.memset(four[:], 4.0)
+        make_identity(nc, ident[:])
+
         nc.sync.dma_start(coh_sb[:], coh)
         load_w(0)
+        load_scale_rows(es_tab, e_scales)
         nc.sync.dma_start(offs_sb[:], offs)
-        load_w(1)
         nc.sync.dma_start(spk_sb[:], spk)
-        nc.sync.dma_start(stat_tab[0:1, :], ms[0:1, :])
-        nc.sync.dma_start(stat_tab[1:2, :], isp[0:1, :])
+        load_w(1)
+        load_scale_rows(ds_tab, d_scales)
+        x_tab = [sb([P, T], I32, "x_tab0")]
         nc.sync.dma_start(x_tab[0][:], words(x_words[0]))
+        nc.gpsimd.dma_start(stat_tab[0:2, :], ms[0:2, :])
+        nc.gpsimd.dma_start(stat_tab[2:4, :], isp[0:2, :])
         for q in range(4):
-            nc.sync.dma_start(ds_tab[32 * q : 32 * q + 4, :].bitcast(I32), d_scales[0, 4 * q : 4 * q + 4, :].bitcast(I32))
-        nc.sync.dma_start(x_tab[1][:], words(x_words[1]))
-        nc.sync.dma_start(e_tab[:], words(e_words[0]))
-        nc.sync.dma_start(d_tab[:], words(d_words[0]))
+            nc.sync.dma_start(xs_tab[32 * q : 32 * q + 8, :].bitcast(I32), x_scales[:, 4 * q : 4 * q + 4, :].bitcast(I32))
 
         half = sb([P, 1], F32, "half")
-        nc.scalar.activation(half[:], ident[:, 0:1], ACT.Abs_reciprocal_sqrt, bias=4.0, scale=0.0)
+        nc.scalar.activation(half[:], four[:], ACT.Abs_reciprocal_sqrt)
 
         es_g = sb([P, U], U8, "es_g")
         ds_g = sb([P, V], U8, "ds_g")
@@ -87,24 +86,31 @@ def tile_picked_ysnorm_sym_p_kernel(
         stat_g = sb([P, V], F32, "stat_g")
         nc.vector.tensor_copy(es_g[:], es_tab[:].indirect(coh_sb[:]))
         nc.vector.tensor_copy(ds_g[:], ds_tab[:].indirect(spk_sb[:]))
-        nc.vector.tensor_copy(xs_g[:], xs_tab[:].indirect(offs_sb[:]))
         nc.vector.tensor_copy(stat_g[:], stat_tab[:].indirect(spk_sb[:]))
+        nc.vector.tensor_copy(xs_g[:], xs_tab[:].indirect(offs_sb[:]))
 
         w_codes = [sb([P, H], U32, f"w_codes{o}") for o in range(PASSES)]
-        w_sc = [sb([P, H], U8, f"w_sc{o}") for o in range(PASSES)]
+        w_sc = [sb([P, H], U8, f"w_sc{o}", tag=("es", "stat")[o]) for o in range(PASSES)]
         for o in range(PASSES):
-            w_bf = sb([P, PACK * H], BF16, f"w_bf{o}")
+            w_bf = sb([P, PACK * H], BF16, f"w_bf{o}", tag=f"bf{o}")
             nc.scalar.copy(
-                w_bf[:].rearrange("p (j m r) -> p m r j", j=PACK, r=PACK),
-                w_raw[o][:].rearrange("p r (m j) -> p m r j", j=PACK),
+                w_bf[:].rearrange("p (j m r) -> p m j r", j=PACK, r=PACK),
+                w_raw[o][:].rearrange("p r (m j) -> p m j r", j=PACK),
             )
             nc.vector.quantize_mx(out=w_codes[o][:].bitcast(FP8X4), scales=w_sc[o][:], in_=w_bf[:])
 
-        turned = psum.tile([P, PACK, P], F32, name="turned", tag="h", bufs=2)
+        x_tab.append(sb([P, T], I32, "x_tab1", tag="raw0"))
+        e_tab = sb([P, W], I32, "e_tab", tag="bf0")
+        d_tab = sb([P, G], I32, "d_tab", tag="raw1")
+        nc.sync.dma_start(x_tab[1][:], words(x_words[1]))
+        nc.sync.dma_start(e_tab[:], words(e_words[0]))
+        nc.sync.dma_start(d_tab[:], words(d_words[0]))
+
+        turned = psum.tile([P, PACK, P], F32, name="turned", tag="h", bufs=3)
         for vh in range(2):
             nc.tensor.transpose(turned[:, vh, :], stat_g[:, vh * P : (vh + 1) * P], ident[:])
         cols = sb([P, 4], F32, "cols")
-        nc.scalar.activation(cols[:, 0:2], turned[:, 0:2, 1], ACT.Copy, scale=half[:])
+        nc.scalar.activation(cols[:, 0:2], turned[:, 0:2, 2], ACT.Copy, scale=half[:])
         for vh in range(2):
             nc.scalar.activation(cols[:, 2 + vh : 3 + vh], turned[:, vh, 0:1], ACT.Copy, scale=cols[:, vh : vh + 1])
         spread = psum.tile([P, 2 * V], F32, name="spread")
@@ -114,20 +120,19 @@ def tile_picked_ysnorm_sym_p_kernel(
         nc.scalar.copy(gain[:], spread[:, 0:V])
         shift = spread[:, V : 2 * V]
 
-        x_g = [sb([P, S], U32, f"x_g{o}") for o in range(PASSES)]
+        x_g = [sb([P, S], U32, "x_g0", tag="ds"), sb([P, S], U32, "x_g1")]
         nc.vector.tensor_copy(x_g[0][:], x_tab[0][:].bitcast(U32).indirect(offs_sb[:]))
         for hf in range(2):
             cut = slice(hf * HALF // 16, (hf + 1) * HALF // 16)
             nc.vector.tensor_copy(x_g[1][:, hf * HALF : (hf + 1) * HALF], x_tab[1][:].bitcast(U32).indirect(offs_sb[:, cut]))
         e_g = sb([P, U], U32, "e_g")
-        d_g = sb([P, V], U32, "d_g")
         nc.vector.tensor_copy(e_g[:], e_tab[:].bitcast(U32).indirect(coh_sb[:]))
-        nc.vector.tensor_copy(d_g[:], d_tab[:].bitcast(U32).indirect(spk_sb[:]))
 
         h_codes, h_sc, zs, ys = {}, {}, {}, {}
+        y_ps = [psum.tile([P, 2, V], F32, name=f"y_ps{u}") for u in range(2)]
 
         def hidden(t):
-            h_ps = psum.tile([P, PACK, P], F32, name=f"h_ps{t}", tag="h", bufs=2)
+            h_ps = psum.tile([P, PACK, P], F32, name=f"h_ps{t}", tag="h", bufs=3)
             tok = slice(t * P, (t + 1) * P)
             for j in range(PACK):
                 ch = slice(j * P, (j + 1) * P)
@@ -141,18 +146,21 @@ def tile_picked_ysnorm_sym_p_kernel(
                         start=(o == 0),
                         stop=(o == PASSES - 1),
                     )
-            h_bf = sb([P, P * PACK], BF16, f"h_bf{t}")
+            h_bf = sb([P, P * PACK], BF16, f"h_bf{t}", tag=f"hb{t}")
             nc.scalar.copy(h_bf[:].rearrange("p (n j) -> p n j", j=PACK), h_ps[:].rearrange("p j n -> p n j"))
             h_codes[t] = sb([P, P], U32, f"h_codes{t}")
             h_sc[t] = sb([P, P], U8, f"h_sc{t}")
             nc.vector.quantize_mx(out=h_codes[t][:].bitcast(FP8X4), scales=h_sc[t][:], in_=h_bf[:])
 
         def scores(t):
-            zs[t] = psum.tile([P, U], F32, name=f"z_ps{t}", tag="z", bufs=3)
-            ys[t] = psum.tile([P, V], F32, name=f"y_ps{t}", tag="y", bufs=2)
-            for acc, codes, sc in ((zs[t], e_g, es_g), (ys[t], d_g, ds_g)):
+            if t < 2:
+                zs[t] = psum.tile([P, U], F32, name=f"z_ps{t}")
+            else:
+                zs[t] = psum.tile([P, U], F32, name=f"z_ps{t}", tag="h", bufs=3)
+            ys[t] = y_ps[t // 2][:, t % 2, :]
+            for acc, codes, sc in ((zs[t][:], e_g, es_g), (ys[t], d_g, ds_g)):
                 nc.tensor.matmul_mx(
-                    out=acc[:],
+                    out=acc,
                     lhsT=h_codes[t][:].bitcast(FP8X4),
                     lhsT_scale=h_sc[t][:],
                     rhs=codes[:].bitcast(FP8X4),
@@ -161,25 +169,43 @@ def tile_picked_ysnorm_sym_p_kernel(
                     stop=True,
                 )
 
-        def finish(t):
-            bn = sb([P, 6], F32, f"bn{t}")
-            mv = sb([P, 2], F32, f"mv{t}")
+        def stats(t):
             inv = sb([P, 1], F32, f"inv{t}")
             off = sb([P, 1], F32, f"off{t}")
+            if t in SCALAR_STATS:
+                z_sb = sb([P, U], F32, f"z_sb{t}")
+                sq = sb([P, U], BF16, f"sq{t}")
+                sums = sb([P, 3], F32, f"sums{t}")
+                nc.scalar.activation(z_sb[:], zs[t][:], ACT.Copy, accum_out=sums[:, 0:1])
+                nc.scalar.activation(sums[:, 1:2], sums[:, 0:1], ACT.Copy, scale=-1.0 / U)
+                nc.scalar.activation(sq[:], z_sb[:], ACT.Square, bias=sums[:, 1:2], accum_out=sums[:, 2:3])
+                nc.scalar.activation(inv[:], sums[:, 2:3], ACT.Abs_reciprocal_sqrt, bias=4.0 * EPS, scale=4.0 / U)
+                nc.scalar.activation(off[:], sums[:, 1:2], ACT.Copy, scale=inv[:])
+                off_op = ALU.add
+            else:
+                bn = sb([P, 6], F32, f"bn{t}")
+                mv = sb([P, 2], F32, f"mv{t}")
+                nc.vector.bn_stats(bn[:], zs[t][:])
+                nc.vector.bn_aggr(mv[:], bn[:])
+                nc.scalar.activation(inv[:], mv[:, 1:2], ACT.Abs_reciprocal_sqrt, bias=4.0 * EPS, scale=4.0)
+                nc.scalar.activation(off[:], mv[:, 0:1], ACT.Copy, scale=inv[:])
+                off_op = ALU.subtract
+            return inv, off, off_op
+
+        def finish(t, inv, off, off_op):
             scaled = sb([P, V], F32, f"scaled{t}")
             res = sb([P, V], F32, f"res{t}")
-            nc.vector.bn_stats(bn[:], zs[t][:])
-            nc.vector.bn_aggr(mv[:], bn[:])
-            nc.scalar.activation(inv[:], mv[:, 1:2], ACT.Abs_reciprocal_sqrt, bias=4.0 * EPS, scale=4.0)
-            nc.scalar.activation(off[:], mv[:, 0:1], ACT.Copy, scale=inv[:])
-            nc.vector.scalar_tensor_tensor(scaled[:], gain[:], inv[:], ys[t][:], ALU.add, ALU.mult)
-            nc.vector.scalar_tensor_tensor(res[:], scaled[:], off[:], shift, ALU.subtract, ALU.subtract)
+            nc.vector.scalar_tensor_tensor(scaled[:], gain[:], inv[:], ys[t], ALU.add, ALU.mult)
+            nc.vector.scalar_tensor_tensor(res[:], scaled[:], off[:], shift, off_op, ALU.subtract)
             nc.sync.dma_start(out[t * P : (t + 1) * P, :], res[:])
 
-        for step in range(TILES + 2):
-            if step < TILES:
-                hidden(step)
-            if 1 <= step <= TILES:
-                scores(step - 1)
-            if step >= 2:
-                finish(step - 2)
+        for step in range(TILES):
+            hidden(step)
+            if step == 0:
+                d_g = sb([P, V], U32, "d_g", tag="hb0")
+                nc.vector.tensor_copy(d_g[:], d_tab[:].bitcast(U32).indirect(spk_sb[:]))
+        for t in range(TILES):
+            scores(t)
+        found = [stats(t) for t in range(TILES)]
+        for t in range(TILES):
+            finish(t, *found[t])

@@ -22,7 +22,7 @@ PASSES = K // (P * PACK)
 TILES = S // P
 HALF = S // 2
 EPS = 0.01
-SCALAR_STATS = (2,)
+SCALAR_STATS = (1,)
 
 
 def tile_picked_ysnorm_sym_p_kernel(
@@ -44,7 +44,7 @@ def tile_picked_ysnorm_sym_p_kernel(
         es_tab = sb([P, W], U8, "es_tab", tag="es")
         stat_tab = sb([P, G], F32, "stat_tab", tag="stat")
         ident = sb([P, P], F32, "ident")
-        four = sb([P, 1], F32, "four")
+        four = sb([P, 1], F32, "four", tag="x1")
         ds_tab = sb([P, G], U8, "ds_tab", tag="ds")
 
         def words(dram):
@@ -94,14 +94,14 @@ def tile_picked_ysnorm_sym_p_kernel(
         for o in range(PASSES):
             w_bf = sb([P, PACK * H], BF16, f"w_bf{o}", tag=f"bf{o}")
             nc.scalar.copy(
-                w_bf[:].rearrange("p (j m r) -> p m j r", j=PACK, r=PACK),
-                w_raw[o][:].rearrange("p r (m j) -> p m j r", j=PACK),
+                w_bf[:].rearrange("p (j m r) -> p m r j", j=PACK, r=PACK),
+                w_raw[o][:].rearrange("p r (m j) -> p m r j", j=PACK),
             )
             nc.vector.quantize_mx(out=w_codes[o][:].bitcast(FP8X4), scales=w_sc[o][:], in_=w_bf[:])
 
-        x_tab.append(sb([P, T], I32, "x_tab1", tag="raw0"))
-        e_tab = sb([P, W], I32, "e_tab", tag="bf0")
-        d_tab = sb([P, G], I32, "d_tab", tag="raw1")
+        x_tab.append(sb([P, T], I32, "x_tab1", tag="x1"))
+        e_tab = sb([P, W], I32, "e_tab", tag="raw0")
+        d_tab = sb([P, G], I32, "d_tab", tag="bf0")
         nc.sync.dma_start(x_tab[1][:], words(x_words[1]))
         nc.sync.dma_start(e_tab[:], words(e_words[0]))
         nc.sync.dma_start(d_tab[:], words(d_words[0]))

@@ -131,6 +131,17 @@ def tile_picked_ysnorm_sym_p_kernel(
         h_codes, h_sc, zs, ys = {}, {}, {}, {}
         y_ps = [psum.tile([P, 2, V], F32, name=f"y_ps{u}") for u in range(2)]
 
+        for rep in range(3):
+            nc.tensor.matmul_mx(
+                out=y_ps[1][:].rearrange("p u v -> p (u v)"),
+                lhsT=w_codes[1][:, 0:P].bitcast(FP8X4),
+                lhsT_scale=w_sc[1][:, 0:P],
+                rhs=w_codes[1][:].bitcast(FP8X4),
+                rhs_scale=w_sc[1][:],
+                start=True,
+                stop=True,
+            )
+
         def hidden(t):
             h_ps = psum.tile([P, PACK, P], F32, name=f"h_ps{t}", tag="h", bufs=3)
             tok = slice(t * P, (t + 1) * P)

from contextlib import ExitStack

import concourse.mybir as mybir
from concourse.masks import make_identity

K, T, S, H, V, W, G, U = 1024, 2048, 512, 512, 256, 1024, 1024, 512
FLOPS = 2 * K * H * S + 2 * H * S * (V + U)

F32 = mybir.dt.float32
BF16 = mybir.dt.bfloat16
I32 = mybir.dt.int32
U32 = mybir.dt.uint32
U16 = mybir.dt.uint16
U8 = mybir.dt.uint8
FP8X4 = mybir.dt.float8_e4m3fn_x4
ACT = mybir.ActivationFunctionType
ALU = mybir.AluOpType

P = 128
PACK = 4
PASSES = K // (P * PACK)
TILES = S // P
HALF = S // 2
EPS = 0.01
SCALAR_STATS = (1,)


def tile_picked_ysnorm_sym_p_kernel(
    tc, x_words, x_scales, w1, e_words, e_scales, d_words, d_scales, ms, isp, offs, coh, spk, out
):
    nc = tc.nc
    with ExitStack() as ctx:
        keep = ctx.enter_context(tc.tile_pool(name="keep", bufs=1))
        psum = ctx.enter_context(tc.psum_pool(name="psum", bufs=1))

        def sb(shape, dtype, name, tag=None):
            return keep.tile(shape, dtype, name=name, tag=tag or name, align_bytes=64)

        offs_sb = keep.tile([P, S // 16], U16, name="offs_sb")
        coh_sb = keep.tile([P, U // 16], U16, name="coh_sb")
        spk_sb = keep.tile([P, V // 16], U16, name="spk_sb")
        w_raw = [sb([P, PACK, H], F32, f"w_raw{o}", tag=f"raw{o}") for o in range(PASSES)]
        xs_tab = sb([P, T], U8, "xs_tab")
        es_tab = sb([P, W], U8, "es_tab", tag="es")
        stat_tab = sb([P, G], F32, "stat_tab", tag="stat")
        ident = sb([P, P], F32, "ident")
        four = sb([P, 1], F32, "four", tag="x1")
        ds_tab = sb([P, G], U8, "ds_tab", tag="ds")

        def words(dram):
            return dram.rearrange("p n t -> p (n t)").bitcast(I32)

        def load_w(o):
            nc.sync.dma_start(w_raw[o][:], w1[512 * o : 512 * (o + 1), :].rearrange("(p r) c -> p r c", r=PACK))

        def load_scale_rows(tab, scales):
            for q in range(4):
                rows = scales[0, 4 * q : 4 * q + 4, :].bitcast(I32)
                nc.sync.dma_start(tab[32 * q : 32 * q + 32, :].bitcast(I32), rows.unsqueeze(0).broadcast_to([8, 4, W // 4]))

        nc.vector.memset(stat_tab[:], 0.0)
        nc.vector.memset(xs_tab[:].bitcast(I32), 0)
        nc.vector.memset(four[:], 4.0)
        make_identity(nc, ident[:])

        nc.sync.dma_start(coh_sb[:], coh)
        load_w(0)
        load_scale_rows(es_tab, e_scales)
        nc.sync.dma_start(offs_sb[:], offs)
        nc.sync.dma_start(spk_sb[:], spk)
        load_w(1)
        load_scale_rows(ds_tab, d_scales)
        x_tab = [sb([P, T], I32, "x_tab0")]
        nc.sync.dma_start(x_tab[0][:], words(x_words[0]))
        nc.gpsimd.dma_start(stat_tab[0:2, :], ms[0:2, :])
        nc.gpsimd.dma_start(stat_tab[2:4, :], isp[0:2, :])
        for q in range(4):
            nc.sync.dma_start(xs_tab[32 * q : 32 * q + 8, :].bitcast(I32), x_scales[:, 4 * q : 4 * q + 4, :].bitcast(I32))

        half = sb([P, 1], F32, "half")
        nc.scalar.activation(half[:], four[:], ACT.Abs_reciprocal_sqrt)

        es_g = sb([P, U], U8, "es_g")
        ds_g = sb([P, V], U8, "ds_g")
        xs_g = sb([P, S], U8, "xs_g")
        stat_g = sb([P, V], F32, "stat_g")
        nc.vector.tensor_copy(es_g[:], es_tab[:].indirect(coh_sb[:]))
        nc.vector.tensor_copy(ds_g[:], ds_tab[:].indirect(spk_sb[:]))
        nc.vector.tensor_copy(stat_g[:], stat_tab[:].indirect(spk_sb[:]))
        nc.vector.tensor_copy(xs_g[:], xs_tab[:].indirect(offs_sb[:]))

        w_codes = [sb([P, H], U32, f"w_codes{o}") for o in range(PASSES)]
        w_sc = [sb([P, H], U8, f"w_sc{o}", tag=("es", "stat")[o]) for o in range(PASSES)]
        for o in range(PASSES):
            w_bf = sb([P, PACK * H], BF16, f"w_bf{o}", tag=f"bf{o}")
            nc.scalar.copy(
                w_bf[:].rearrange("p (j m r) -> p m r j", j=PACK, r=PACK),
                w_raw[o][:].rearrange("p r (m j) -> p m r j", j=PACK),
            )
            nc.vector.quantize_mx(out=w_codes[o][:].bitcast(FP8X4), scales=w_sc[o][:], in_=w_bf[:])

        x_tab.append(sb([P, T], I32, "x_tab1", tag="x1"))
        e_tab = sb([P, W], I32, "e_tab", tag="raw0")
        d_tab = sb([P, G], I32, "d_tab", tag="bf0")
        nc.sync.dma_start(x_tab[1][:], words(x_words[1]))
        nc.sync.dma_start(e_tab[:], words(e_words[0]))
        nc.sync.dma_start(d_tab[:], words(d_words[0]))

        turned = psum.tile([P, PACK, P], F32, name="turned", tag="h", bufs=3)
        for vh in range(2):
            nc.tensor.transpose(turned[:, vh, :], stat_g[:, vh * P : (vh + 1) * P], ident[:])
        cols = sb([P, 4], F32, "cols")
        nc.scalar.activation(cols[:, 0:2], turned[:, 0:2, 2], ACT.Copy, scale=half[:])
        for vh in range(2):
            nc.scalar.activation(cols[:, 2 + vh : 3 + vh], turned[:, vh, 0:1], ACT.Copy, scale=cols[:, vh : vh + 1])
        spread = psum.tile([P, 2 * V], F32, name="spread")
        for c in range(4):
            nc.tensor.transpose(spread[:, c * P : (c + 1) * P], cols[:, c : c + 1].to_broadcast([P, P]), ident[:])
        gain = sb([P, V], F32, "gain")
        nc.scalar.copy(gain[:], spread[:, 0:V])
        shift = spread[:, V : 2 * V]

        x_g = [sb([P, S], U32, "x_g0", tag="ds"), sb([P, S], U32, "x_g1")]
        nc.vector.tensor_copy(x_g[0][:], x_tab[0][:].bitcast(U32).indirect(offs_sb[:]))
        for hf in range(2):
            cut = slice(hf * HALF // 16, (hf + 1) * HALF // 16)
            nc.vector.tensor_copy(x_g[1][:, hf * HALF : (hf + 1) * HALF], x_tab[1][:].bitcast(U32).indirect(offs_sb[:, cut]))
        e_g = sb([P, U], U32, "e_g")
        nc.vector.tensor_copy(e_g[:], e_tab[:].bitcast(U32).indirect(coh_sb[:]))

        h_codes, h_sc, zs, ys = {}, {}, {}, {}
        y_ps = [psum.tile([P, 2, V], F32, name=f"y_ps{u}") for u in range(2)]

        for rep in range(3):
            nc.tensor.matmul_mx(
                out=y_ps[1][:].rearrange("p u v -> p (u v)"),
                lhsT=w_codes[1][:, 0:P].bitcast(FP8X4),
                lhsT_scale=w_sc[1][:, 0:P],
                rhs=w_codes[1][:].bitcast(FP8X4),
                rhs_scale=w_sc[1][:],
                start=True,
                stop=True,
            )

        def hidden(t):
            h_ps = psum.tile([P, PACK, P], F32, name=f"h_ps{t}", tag="h", bufs=3)
            tok = slice(t * P, (t + 1) * P)
            for j in range(PACK):
                ch = slice(j * P, (j + 1) * P)
                for o in range(PASSES):
                    nc.tensor.matmul_mx(
                        out=h_ps[:, j, :],
                        lhsT=w_codes[o][:, ch].bitcast(FP8X4),
                        lhsT_scale=w_sc[o][:, ch],
                        rhs=x_g[o][:, tok].bitcast(FP8X4),
                        rhs_scale=xs_g[4 * o : P, tok],
                        start=(o == 0),
                        stop=(o == PASSES - 1),
                    )
            h_bf = sb([P, P * PACK], BF16, f"h_bf{t}", tag=f"hb{t}")
            nc.scalar.copy(h_bf[:].rearrange("p (n j) -> p n j", j=PACK), h_ps[:].rearrange("p j n -> p n j"))
            h_codes[t] = sb([P, P], U32, f"h_codes{t}")
            h_sc[t] = sb([P, P], U8, f"h_sc{t}")
            nc.vector.quantize_mx(out=h_codes[t][:].bitcast(FP8X4), scales=h_sc[t][:], in_=h_bf[:])

        def scores(t):
            if t < 2:
                zs[t] = psum.tile([P, U], F32, name=f"z_ps{t}")
            else:
                zs[t] = psum.tile([P, U], F32, name=f"z_ps{t}", tag="h", bufs=3)
            ys[t] = y_ps[t // 2][:, t % 2, :]
            for acc, codes, sc in ((zs[t][:], e_g, es_g), (ys[t], d_g, ds_g)):
                nc.tensor.matmul_mx(
                    out=acc,
                    lhsT=h_codes[t][:].bitcast(FP8X4),
                    lhsT_scale=h_sc[t][:],
                    rhs=codes[:].bitcast(FP8X4),
                    rhs_scale=sc[:],
                    start=True,
                    stop=True,
                )

        def stats(t):
            inv = sb([P, 1], F32, f"inv{t}")
            off = sb([P, 1], F32, f"off{t}")
            if t in SCALAR_STATS:
                z_sb = sb([P, U], F32, f"z_sb{t}")
                sq = sb([P, U], BF16, f"sq{t}")
                sums = sb([P, 3], F32, f"sums{t}")
                nc.scalar.activation(z_sb[:], zs[t][:], ACT.Copy, accum_out=sums[:, 0:1])
                nc.scalar.activation(sums[:, 1:2], sums[:, 0:1], ACT.Copy, scale=-1.0 / U)
                nc.scalar.activation(sq[:], z_sb[:], ACT.Square, bias=sums[:, 1:2], accum_out=sums[:, 2:3])
                nc.scalar.activation(inv[:], sums[:, 2:3], ACT.Abs_reciprocal_sqrt, bias=4.0 * EPS, scale=4.0 / U)
                nc.scalar.activation(off[:], sums[:, 1:2], ACT.Copy, scale=inv[:])
                off_op = ALU.add
            else:
                bn = sb([P, 6], F32, f"bn{t}")
                mv = sb([P, 2], F32, f"mv{t}")
                nc.vector.bn_stats(bn[:], zs[t][:])
                nc.vector.bn_aggr(mv[:], bn[:])
                nc.scalar.activation(inv[:], mv[:, 1:2], ACT.Abs_reciprocal_sqrt, bias=4.0 * EPS, scale=4.0)
                nc.scalar.activation(off[:], mv[:, 0:1], ACT.Copy, scale=inv[:])
                off_op = ALU.subtract
            return inv, off, off_op

        def finish(t, inv, off, off_op):
            scaled = sb([P, V], F32, f"scaled{t}")
            res = sb([P, V], F32, f"res{t}")
            nc.vector.scalar_tensor_tensor(scaled[:], gain[:], inv[:], ys[t], ALU.add, ALU.mult)
            nc.vector.scalar_tensor_tensor(res[:], scaled[:], off[:], shift, off_op, ALU.subtract)
            nc.sync.dma_start(out[t * P : (t + 1) * P, :], res[:])

        for step in range(TILES):
            hidden(step)
            if step == 0:
                d_g = sb([P, V], U32, "d_g", tag="hb0")
                nc.vector.tensor_copy(d_g[:], d_tab[:].bitcast(U32).indirect(spk_sb[:]))
        for t in range(TILES):
            scores(t)
        found = [stats(t) for t in range(TILES)]
        for t in range(TILES):
            finish(t, *found[t])
